import numpy as np
import ml_dtypes


def mxq(x, axis, fmt="e4m3"):
    dtype, down = {"e4m3": (ml_dtypes.float8_e4m3fn, 7), "e5m2": (ml_dtypes.float8_e5m2, 14)}[fmt]
    v = np.moveaxis(np.asarray(x, np.float32).astype(ml_dtypes.bfloat16).astype(np.float64), axis, -1)
    blocks = v.reshape(v.shape[:-1] + (-1, 32))
    amax = np.abs(blocks).max(-1, keepdims=True)
    byte = np.maximum(np.where(amax > 0, np.frexp(amax)[1] - 1 + 127, 0) - down, 1)
    scale = np.exp2(byte - 127.0)
    codes = (blocks / scale).astype(np.float32).astype(dtype).astype(np.float64)
    return np.moveaxis((codes * scale).reshape(v.shape), -1, axis)


WIDE = False


def mx_kscale(k):
    if not WIDE:
        return np.ones(k)
    levels = np.array([10, -10, 5, -5, 0])
    if k % 512:
        return np.exp2(np.random.permutation(np.resize(levels, k // 32))).repeat(32)
    a = np.empty((k // 512, 16))
    for p in range(k // 512):
        a[p, :8] = np.random.permutation(np.resize(levels, 8))
        for g in range(8):
            far = levels[np.abs(levels - a[p, g]) >= 10]
            a[p, g + 8] = far[np.random.randint(len(far))]
    return np.exp2(a.ravel()).repeat(32)


def f64(x):
    return np.asarray(x).astype(np.float64)


def striped(idx):
    return np.tile(np.asarray(idx).reshape(-1, 16).T, (8, 1)).astype(np.uint16)


def unstriped(offs):
    return offs[:16].T.reshape(-1).astype(np.int64)


E2M1 = np.array([0.0, 0.5, 1.0, 1.5, 2.0, 3.0, 4.0, 6.0, -0.0, -0.5, -1.0, -1.5, -2.0, -3.0, -4.0, -6.0])


def pack_weight(w, fmt):
    k, n = w.shape
    w = f64(np.asarray(w, np.float32).astype(ml_dtypes.bfloat16)).reshape(k // 32, 32, n)
    amax = np.abs(w).max(1)
    if fmt == "e4m3":
        byte = np.frexp(amax)[1] - 1 + 127 - 7
    else:
        mant, ex = np.frexp(amax / 6.0)
        byte = np.where(mant > 0.5, ex, ex - 1) + 127
    byte = np.clip(np.where(amax > 0, byte, 1), 1, 254)
    scaled = (w * np.exp2(127.0 - byte)[:, None, :]).reshape(k, n).astype(np.float32)
    by_word = np.ascontiguousarray(scaled.reshape(k // 512, 128, 4, n).transpose(0, 1, 3, 2))
    if fmt == "e4m3":
        words = by_word.astype(ml_dtypes.float8_e4m3fn).view(np.uint8)
    else:
        c = by_word.astype(ml_dtypes.float4_e2m1fn).view(np.uint8) & 0xF
        words = (c[..., 0::2] | (c[..., 1::2] << 4)).reshape(k // 512, 128, 2 * n)
    return np.ascontiguousarray(words), np.ascontiguousarray(byte.astype(np.uint8).reshape(k // 512, 16, n))


def unpack_weight(words, scales, fmt):
    g, _, n = scales.shape
    words = np.ascontiguousarray(words).reshape(g, 128, n, -1)
    if fmt == "e4m3":
        vals = words.view(ml_dtypes.float8_e4m3fn).astype(np.float64)
    else:
        nib = np.empty((g, 128, n, 4), np.uint8)
        nib[..., 0::2] = words & 0xF
        nib[..., 1::2] = words >> 4
        vals = E2M1[nib]
    vals = vals * np.repeat(np.exp2(scales.astype(np.float64) - 127.0), 8, axis=1)[..., None]
    return vals.transpose(0, 1, 3, 2).reshape(g * 512, n)


def sigmoid(v):
    return 1.0 / (1.0 + np.exp(-v))


B, N, T, D, NQ = 1, 512, 2048, 1024, 128


def setup_inputs():
    n = np.random.standard_normal
    idx = np.random.permutation(T)[:B * N]
    s = mx_kscale(D)[:, None]
    kp = pack_weight(n((D, T)) / s, "e2m1")
    cp = pack_weight(n((D, T)) / s / 12, "e2m1")
    return {
        "qT": (n((B, D, NQ)) * s * (1.00 / np.sqrt(D))).astype(np.float32),
        "k_words": np.ascontiguousarray(kp[0].reshape(1, 2, 128, T, 2).transpose(0, 2, 3, 1, 4)).reshape(1, 128, T, 4),
        "k_scales": kp[1],
        "c_words": np.ascontiguousarray(cp[0].reshape(1, 2, 128, T, 2).transpose(0, 2, 3, 1, 4)).reshape(1, 128, T, 4),
        "c_scales": cp[1],
        "offs": striped(idx),
    }


def reference(qT, k_words, k_scales, c_words, c_scales, offs):
    idx = unstriped(offs)
    pick = lambda x, which: x[:, which].reshape(x.shape[0], B, -1).transpose(1, 0, 2)
    k = unpack_weight(k_words.reshape(1, 128, T, 2, 2).transpose(0, 3, 1, 2, 4).reshape(2, 128, 2 * T), k_scales, "e2m1")
    kg = pick(k, idx)
    c = unpack_weight(c_words.reshape(1, 128, T, 2, 2).transpose(0, 3, 1, 2, 4).reshape(2, 128, 2 * T), c_scales, "e2m1")
    cg = pick(c, idx)
    qq = mxq(f64(qT), 1, "e4m3")
    a = (qq.transpose(0, 2, 1) @ kg) + (qq.transpose(0, 2, 1) @ cg)
    y = sigmoid(a)
    out = np.zeros((B, NQ, T))
    for b in range(B):
        out[b][:, idx[b * N:(b + 1) * N]] = y[b]
    return out

@@ -1,0 +1,106 @@
+from contextlib import ExitStack
+
+import concourse.mybir as mybir
+
+F32 = mybir.dt.float32
+BF16 = mybir.dt.bfloat16
+I32 = mybir.dt.int32
+U32 = mybir.dt.uint32
+U16 = mybir.dt.uint16
+U8 = mybir.dt.uint8
+FP8X4 = mybir.dt.float8_e4m3fn_x4
+FP4X4 = mybir.dt.float4_e2m1fn_x4
+SIGMOID = mybir.ActivationFunctionType.Sigmoid
+
+P = 128
+T = 2048
+N = 512
+NQ = 128
+D = 1024
+FLOPS = 2 * 2 * D * NQ * N
+HALF = N // 2
+G = 128
+
+
+def tile_attend_residscat_topk_kernel(tc, qT, k_words, k_scales, c_words, c_scales, offs, out):
+    nc = tc.nc
+    with ExitStack() as ctx:
+        keep = ctx.enter_context(tc.tile_pool(name="keep", bufs=1))
+        psum = ctx.enter_context(tc.psum_pool(name="psum", bufs=1))
+
+        offsets = keep.tile([P, N // 16], U16, name="offsets")
+        nc.sync.dma_start(offsets[:], offs)
+
+        kw = keep.tile([P, T], I32, name="kw")
+        cw = keep.tile([P, T], I32, name="cw")
+        q_raw = keep.tile([P, 2, 4, NQ], F32, name="q_raw")
+        s_wins = []
+        for name, scales in (("ks_win", k_scales), ("cs_win", c_scales)):
+            win = keep.tile([P, T], U8, name=name)
+            nc.sync.dma_start(win[0:32, :].bitcast(I32), scales.rearrange("o f t -> (o f) t").bitcast(I32))
+            nc.vector.memset(win[32:64, :].bitcast(I32), 0)
+            nc.vector.memset(win[64:128, :].bitcast(I32), 0)
+            s_wins.append(win)
+        nc.scalar.dma_start(kw[:], k_words[0].rearrange("p t b -> p (t b)").bitcast(I32))
+        nc.scalar.dma_start(q_raw[:], qT[0].rearrange("(o p j) n -> p o j n", o=2, j=4))
+        nc.scalar.dma_start(cw[:], c_words[0].rearrange("p t b -> p (t b)").bitcast(I32))
+
+        warm = keep.tile([P, 2], F32, name="warm")
+        nc.gpsimd.memset(warm[:, 0:1], 0.0)
+        nc.scalar.activation(warm[:, 1:2], warm[:, 0:1], SIGMOID)
+        planes = keep.tile([P, 2, 2 * N], U8, name="planes", align_bytes=64)
+        nc.vector.memset(planes[:].rearrange("p o n -> p (o n)").bitcast(I32), 0)
+        window = keep.tile([P, T], F32, name="window")
+        nc.vector.memset(window[:], 0.0)
+
+        s_g = keep.tile([P, 2 * N], U8, name="s_g", align_bytes=64)
+        for i in range(2):
+            nc.vector.tensor_copy(s_g[:, i * N : (i + 1) * N], s_wins[i][:].indirect(offsets[:]))
+        for o in range(2):
+            for Q in range(4):
+                if o == 0 and Q == 0:
+                    nc.vector.tensor_copy(planes[0:32, 0, :].bitcast(I32), s_g[0:32, :].bitcast(I32))
+                else:
+                    nc.sync.dma_start(planes[32 * Q : 32 * Q + 4, o, :].bitcast(I32),
+                                      s_g[16 * o + 4 * Q : 16 * o + 4 * Q + 4, :].bitcast(I32))
+
+        q_bf = keep.tile([P, 2, NQ, 4], BF16, name="q_bf", align_bytes=64)
+        for o in range(2):
+            nc.scalar.copy(q_bf[:, o], q_raw[:, o].rearrange("p j n -> p n j"))
+        q_codes = keep.tile([P, 2 * NQ], U32, name="q_codes", align_bytes=64)
+        q_plane = keep.tile([P, 2 * NQ], U8, name="q_plane", align_bytes=64)
+
+        k_g = keep.tile([P, N], U32, name="k_g")
+        nc.vector.tensor_copy(k_g[:], kw[:].bitcast(U32).indirect(offsets[:]))
+        k_split = keep.tile([P, 2, 2 * N], U8, name="k_split", align_bytes=64)
+        nc.vector.tensor_copy(k_split[:].bitcast(U16), k_g[:].bitcast(U16).rearrange("p (n h) -> p h n", h=2))
+        nc.vector.quantize_mx(q_codes[:].bitcast(FP8X4), q_plane[:], q_bf[:].rearrange("p o n j -> p (o n j)"))
+
+        banks = [psum.tile([P, G], F32, name="bank%d" % g) for g in range(4)]
+        for g in range(4):
+            for o in range(2):
+                nc.tensor.matmul_mx(banks[g][:], lhsT=q_codes[:, o * NQ : (o + 1) * NQ].bitcast(FP8X4),
+                                    lhsT_scale=q_plane[:, o * NQ : (o + 1) * NQ],
+                                    rhs=k_split[:, o, 2 * G * g : 2 * G * (g + 1)].bitcast(FP4X4),
+                                    rhs_scale=planes[:, o, G * g : G * (g + 1)],
+                                    start=(o == 0), stop=False)
+        ys = []
+        for h in range(2):
+            c_g = keep.tile([P, HALF], U32, name="c_g%d" % h)
+            nc.vector.tensor_copy(c_g[:], cw[:].bitcast(U32).indirect(offsets[:, 16 * h : 16 * (h + 1)]))
+            c_split = keep.tile([P, 2, 2 * HALF], U8, name="c_split%d" % h, align_bytes=64)
+            nc.vector.tensor_copy(c_split[:].bitcast(U16), c_g[:].bitcast(U16).rearrange("p (n h) -> p h n", h=2))
+            y = keep.tile([P, HALF], F32, name="y%d" % h)
+            for j in range(2):
+                g = 2 * h + j
+                for o in range(2):
+                    nc.tensor.matmul_mx(banks[g][:], lhsT=q_codes[:, o * NQ : (o + 1) * NQ].bitcast(FP8X4),
+                                        lhsT_scale=q_plane[:, o * NQ : (o + 1) * NQ],
+                                        rhs=c_split[:, o, 2 * G * j : 2 * G * (j + 1)].bitcast(FP4X4),
+                                        rhs_scale=planes[:, o, N + G * g : N + G * (g + 1)],
+                                        start=False, stop=(o == 1))
+                nc.scalar.activation(y[:, G * j : G * (j + 1)], banks[g][:], SIGMOID)
+            ys.append(y)
+        for h in range(2):
+            nc.vector.tensor_copy(window[:].indirect(offsets[:, 16 * h : 16 * (h + 1)]), ys[h][:])
+        nc.sync.dma_start(out[0], window[:])

@@ -41,9 +41,9 @@ def tile_attend_residscat_topk_kernel(tc, qT, k_words, k_scales, c_words, c_scal
             nc.vector.memset(win[32:64, :].bitcast(I32), 0)
             nc.vector.memset(win[64:128, :].bitcast(I32), 0)
             s_wins.append(win)
-        nc.scalar.dma_start(kw[:], k_words[0].rearrange("p t b -> p (t b)").bitcast(I32))
-        nc.scalar.dma_start(q_raw[:], qT[0].rearrange("(o p j) n -> p o j n", o=2, j=4))
-        nc.scalar.dma_start(cw[:], c_words[0].rearrange("p t b -> p (t b)").bitcast(I32))
+        nc.sync.dma_start(kw[:], k_words[0].rearrange("p t b -> p (t b)").bitcast(I32))
+        nc.sync.dma_start(q_raw[:], qT[0].rearrange("(o p j) n -> p o j n", o=2, j=4))
+        nc.sync.dma_start(cw[:], c_words[0].rearrange("p t b -> p (t b)").bitcast(I32))
 
         warm = keep.tile([P, 2], F32, name="warm")
         nc.gpsimd.memset(warm[:, 0:1], 0.0)
@@ -51,7 +51,7 @@ def tile_attend_residscat_topk_kernel(tc, qT, k_words, k_scales, c_words, c_scal
         planes = keep.tile([P, 2, 2 * N], U8, name="planes", align_bytes=64)
         nc.vector.memset(planes[:].rearrange("p o n -> p (o n)").bitcast(I32), 0)
         window = keep.tile([P, T], F32, name="window")
-        nc.vector.memset(window[:], 0.0)
+        nc.gpsimd.memset(window[:], 0.0)
 
         s_g = keep.tile([P, 2 * N], U8, name="s_g", align_bytes=64)
         for i in range(2):
@@ -61,7 +61,7 @@ def tile_attend_residscat_topk_kernel(tc, qT, k_words, k_scales, c_words, c_scal
                 if o == 0 and Q == 0:
                     nc.vector.tensor_copy(planes[0:32, 0, :].bitcast(I32), s_g[0:32, :].bitcast(I32))
                 else:
-                    nc.sync.dma_start(planes[32 * Q : 32 * Q + 4, o, :].bitcast(I32),
+                    nc.scalar.dma_start(planes[32 * Q : 32 * Q + 4, o, :].bitcast(I32),
                                       s_g[16 * o + 4 * Q : 16 * o + 4 * Q + 4, :].bitcast(I32))
 
         q_bf = keep.tile([P, 2, NQ, 4], BF16, name="q_bf", align_bytes=64)
@@ -77,16 +77,16 @@ def tile_attend_residscat_topk_kernel(tc, qT, k_words, k_scales, c_words, c_scal
         nc.vector.quantize_mx(q_codes[:].bitcast(FP8X4), q_plane[:], q_bf[:].rearrange("p o n j -> p (o n j)"))
 
         banks = [psum.tile([P, G], F32, name="bank%d" % g) for g in range(4)]
-        for g in range(4):
-            for o in range(2):
-                nc.tensor.matmul_mx(banks[g][:], lhsT=q_codes[:, o * NQ : (o + 1) * NQ].bitcast(FP8X4),
-                                    lhsT_scale=q_plane[:, o * NQ : (o + 1) * NQ],
-                                    rhs=k_split[:, o, 2 * G * g : 2 * G * (g + 1)].bitcast(FP4X4),
-                                    rhs_scale=planes[:, o, G * g : G * (g + 1)],
-                                    start=(o == 0), stop=False)
+        c_g = keep.tile([P, HALF], U32, name="c_g")
         ys = []
         for h in range(2):
-            c_g = keep.tile([P, HALF], U32, name="c_g%d" % h)
+            for g in (2 * h, 2 * h + 1):
+                for o in range(2):
+                    nc.tensor.matmul_mx(banks[g][:], lhsT=q_codes[:, o * NQ : (o + 1) * NQ].bitcast(FP8X4),
+                                        lhsT_scale=q_plane[:, o * NQ : (o + 1) * NQ],
+                                        rhs=k_split[:, o, 2 * G * g : 2 * G * (g + 1)].bitcast(FP4X4),
+                                        rhs_scale=planes[:, o, G * g : G * (g + 1)],
+                                        start=(o == 0), stop=False)
             nc.vector.tensor_copy(c_g[:], cw[:].bitcast(U32).indirect(offsets[:, 16 * h : 16 * (h + 1)]))
             c_split = keep.tile([P, 2, 2 * HALF], U8, name="c_split%d" % h, align_bytes=64)
             nc.vector.tensor_copy(c_split[:].bitcast(U16), c_g[:].bitcast(U16).rearrange("p (n h) -> p h n", h=2))

@@ -34,6 +34,7 @@ def tile_attend_residscat_topk_kernel(tc, qT, k_words, k_scales, c_words, c_scal
         kw = keep.tile([P, T], I32, name="kw")
         cw = keep.tile([P, T], I32, name="cw")
         q_raw = keep.tile([P, 2, 4, NQ], F32, name="q_raw")
+        nc.scalar.dma_start(q_raw[:], qT[0].rearrange("(o p j) n -> p o j n", o=2, j=4))
         s_wins = []
         for name, scales in (("ks_win", k_scales), ("cs_win", c_scales)):
             win = keep.tile([P, T], U8, name=name)
@@ -42,27 +43,25 @@ def tile_attend_residscat_topk_kernel(tc, qT, k_words, k_scales, c_words, c_scal
             nc.vector.memset(win[64:128, :].bitcast(I32), 0)
             s_wins.append(win)
         nc.sync.dma_start(kw[:], k_words[0].rearrange("p t b -> p (t b)").bitcast(I32))
-        nc.sync.dma_start(q_raw[:], qT[0].rearrange("(o p j) n -> p o j n", o=2, j=4))
         nc.sync.dma_start(cw[:], c_words[0].rearrange("p t b -> p (t b)").bitcast(I32))
 
         warm = keep.tile([P, 2], F32, name="warm")
         nc.gpsimd.memset(warm[:, 0:1], 0.0)
         nc.scalar.activation(warm[:, 1:2], warm[:, 0:1], SIGMOID)
         planes = keep.tile([P, 2, 2 * N], U8, name="planes", align_bytes=64)
-        nc.vector.memset(planes[:].rearrange("p o n -> p (o n)").bitcast(I32), 0)
+        nc.vector.memset(planes[:, 1, :].bitcast(I32), 0)
         window = keep.tile([P, T], F32, name="window")
-        nc.gpsimd.memset(window[:], 0.0)
+        for i in range(8):
+            nc.gpsimd.memset(window[:, 256 * i : 256 * (i + 1)], 0.0)
 
         s_g = keep.tile([P, 2 * N], U8, name="s_g", align_bytes=64)
         for i in range(2):
             nc.vector.tensor_copy(s_g[:, i * N : (i + 1) * N], s_wins[i][:].indirect(offsets[:]))
-        for o in range(2):
-            for Q in range(4):
-                if o == 0 and Q == 0:
-                    nc.vector.tensor_copy(planes[0:32, 0, :].bitcast(I32), s_g[0:32, :].bitcast(I32))
-                else:
-                    nc.scalar.dma_start(planes[32 * Q : 32 * Q + 4, o, :].bitcast(I32),
-                                      s_g[16 * o + 4 * Q : 16 * o + 4 * Q + 4, :].bitcast(I32))
+        nc.vector.tensor_copy(planes[:, 0, :].bitcast(I32), s_g[:].bitcast(I32))
+        for o in (1, 0):
+            for Q in range(1 - o, 4):
+                nc.sync.dma_start(planes[32 * Q : 32 * Q + 4, o, :].bitcast(I32),
+                                  s_g[16 * o + 4 * Q : 16 * o + 4 * Q + 4, :].bitcast(I32))
 
         q_bf = keep.tile([P, 2, NQ, 4], BF16, name="q_bf", align_bytes=64)
         for o in range(2):
@@ -76,30 +75,34 @@ def tile_attend_residscat_topk_kernel(tc, qT, k_words, k_scales, c_words, c_scal
         nc.vector.tensor_copy(k_split[:].bitcast(U16), k_g[:].bitcast(U16).rearrange("p (n h) -> p h n", h=2))
         nc.vector.quantize_mx(q_codes[:].bitcast(FP8X4), q_plane[:], q_bf[:].rearrange("p o n j -> p (o n j)"))
 
-        banks = [psum.tile([P, G], F32, name="bank%d" % g) for g in range(4)]
+        pair = [psum.tile([P, 2, G], F32, name="bank%d" % j) for j in range(2)]
+        banks = [pair[g % 2][:, g // 2, :] for g in range(4)]
         c_g = keep.tile([P, HALF], U32, name="c_g")
+
+        def passes(g, words, col, plane_col, first):
+            for o in (1, 0):
+                nc.tensor.matmul_mx(banks[g], lhsT=q_codes[:, o * NQ : (o + 1) * NQ].bitcast(FP8X4),
+                                    lhsT_scale=q_plane[:, o * NQ : (o + 1) * NQ],
+                                    rhs=words[:, o, 2 * col : 2 * (col + G)].bitcast(FP4X4),
+                                    rhs_scale=planes[:, o, plane_col : plane_col + G],
+                                    start=(first and o == 1), stop=(not first and o == 0))
+
         ys = []
         for h in range(2):
             for g in (2 * h, 2 * h + 1):
-                for o in range(2):
-                    nc.tensor.matmul_mx(banks[g][:], lhsT=q_codes[:, o * NQ : (o + 1) * NQ].bitcast(FP8X4),
-                                        lhsT_scale=q_plane[:, o * NQ : (o + 1) * NQ],
-                                        rhs=k_split[:, o, 2 * G * g : 2 * G * (g + 1)].bitcast(FP4X4),
-                                        rhs_scale=planes[:, o, G * g : G * (g + 1)],
-                                        start=(o == 0), stop=False)
+                passes(g, k_split, G * g, G * g, True)
             nc.vector.tensor_copy(c_g[:], cw[:].bitcast(U32).indirect(offsets[:, 16 * h : 16 * (h + 1)]))
             c_split = keep.tile([P, 2, 2 * HALF], U8, name="c_split%d" % h, align_bytes=64)
-            nc.vector.tensor_copy(c_split[:].bitcast(U16), c_g[:].bitcast(U16).rearrange("p (n h) -> p h n", h=2))
+            pieces = 2 - h
+            for j in range(pieces):
+                w = HALF // pieces
+                nc.vector.tensor_copy(c_split[:, :, 2 * w * j : 2 * w * (j + 1)].bitcast(U16),
+                                      c_g[:, w * j : w * (j + 1)].bitcast(U16).rearrange("p (n h) -> p h n", h=2))
             y = keep.tile([P, HALF], F32, name="y%d" % h)
             for j in range(2):
                 g = 2 * h + j
-                for o in range(2):
-                    nc.tensor.matmul_mx(banks[g][:], lhsT=q_codes[:, o * NQ : (o + 1) * NQ].bitcast(FP8X4),
-                                        lhsT_scale=q_plane[:, o * NQ : (o + 1) * NQ],
-                                        rhs=c_split[:, o, 2 * G * j : 2 * G * (j + 1)].bitcast(FP4X4),
-                                        rhs_scale=planes[:, o, N + G * g : N + G * (g + 1)],
-                                        start=False, stop=(o == 1))
-                nc.scalar.activation(y[:, G * j : G * (j + 1)], banks[g][:], SIGMOID)
+                passes(g, c_split, G * j, N + G * g, False)
+                nc.scalar.activation(y[:, G * j : G * (j + 1)], banks[g], SIGMOID)
             ys.append(y)
         for h in range(2):
             nc.vector.tensor_copy(window[:].indirect(offsets[:, 16 * h : 16 * (h + 1)]), ys[h][:])

@@ -69,15 +69,10 @@ def tile_attend_residscat_topk_kernel(tc, qT, k_words, k_scales, c_words, c_scal
         q_codes = keep.tile([P, 2 * NQ], U32, name="q_codes", align_bytes=64)
         q_plane = keep.tile([P, 2 * NQ], U8, name="q_plane", align_bytes=64)
 
-        k_g = keep.tile([P, N], U32, name="k_g")
-        nc.vector.tensor_copy(k_g[:], kw[:].bitcast(U32).indirect(offsets[:]))
-        k_split = keep.tile([P, 2, 2 * N], U8, name="k_split", align_bytes=64)
-        nc.vector.tensor_copy(k_split[:].bitcast(U16), k_g[:].bitcast(U16).rearrange("p (n h) -> p h n", h=2))
         nc.vector.quantize_mx(q_codes[:].bitcast(FP8X4), q_plane[:], q_bf[:].rearrange("p o n j -> p (o n j)"))
 
         pair = [psum.tile([P, 2, G], F32, name="bank%d" % j) for j in range(2)]
         banks = [pair[g % 2][:, g // 2, :] for g in range(4)]
-        c_g = keep.tile([P, HALF], U32, name="c_g")
 
         def passes(g, words, col, plane_col, first):
             for o in (1, 0):
@@ -87,23 +82,36 @@ def tile_attend_residscat_topk_kernel(tc, qT, k_words, k_scales, c_words, c_scal
                                     rhs_scale=planes[:, o, plane_col : plane_col + G],
                                     start=(first and o == 1), stop=(not first and o == 0))
 
-        ys = []
-        for h in range(2):
-            for g in (2 * h, 2 * h + 1):
-                passes(g, k_split, G * g, G * g, True)
-            nc.vector.tensor_copy(c_g[:], cw[:].bitcast(U32).indirect(offsets[:, 16 * h : 16 * (h + 1)]))
-            c_split = keep.tile([P, 2, 2 * HALF], U8, name="c_split%d" % h, align_bytes=64)
-            pieces = 2 - h
-            for j in range(pieces):
-                w = HALF // pieces
-                nc.vector.tensor_copy(c_split[:, :, 2 * w * j : 2 * w * (j + 1)].bitcast(U16),
-                                      c_g[:, w * j : w * (j + 1)].bitcast(U16).rearrange("p (n h) -> p h n", h=2))
-            y = keep.tile([P, HALF], F32, name="y%d" % h)
-            for j in range(2):
-                g = 2 * h + j
-                passes(g, c_split, G * j, N + G * g, False)
-                nc.scalar.activation(y[:, G * j : G * (j + 1)], banks[g], SIGMOID)
-            ys.append(y)
+        def gather(dst, pool_words, h):
+            nc.vector.tensor_copy(dst, pool_words[:].bitcast(U32).indirect(offsets[:, 16 * h : 16 * (h + 1)]))
+
+        def part(dst, src):
+            nc.vector.tensor_copy(dst.bitcast(U16), src.bitcast(U16).rearrange("p (n h) -> p h n", h=2))
+
+        k_first = keep.tile([P, HALF], U32, name="k_first")
+        late = keep.tile([P, N], U32, name="late")
+        k_split = [keep.tile([P, 2, 2 * HALF], U8, name="k_split%d" % h, align_bytes=64) for h in range(2)]
+        c_split = [keep.tile([P, 2, 2 * HALF], U8, name="c_split%d" % h, align_bytes=64) for h in range(2)]
+        ys = [keep.tile([P, HALF], F32, name="y%d" % h) for h in range(2)]
+
+        gather(k_first[:], kw, 0)
+        part(k_split[0][:], k_first[:])
+        for g in range(2):
+            passes(g, k_split[0], G * g, G * g, True)
+        gather(late[:, G : G + HALF], cw, 0)
+        for g in range(2):
+            part(c_split[0][:, :, 2 * G * g : 2 * G * (g + 1)], late[:, G * (g + 1) : G * (g + 2)])
+            passes(g, c_split[0], G * g, N + G * g, False)
+            nc.scalar.activation(ys[0][:, G * g : G * (g + 1)], banks[g], SIGMOID)
+        gather(late[:, 0:HALF], cw, 1)
+        gather(late[:, HALF:N], kw, 1)
+        part(c_split[1][:], late[:, 0:HALF])
+        part(k_split[1][:], late[:, HALF:N])
+        for j in range(2):
+            passes(2 + j, c_split[1], G * j, N + HALF + G * j, True)
+        for j in range(2):
+            passes(2 + j, k_split[1], G * j, HALF + G * j, False)
+            nc.scalar.activation(ys[1][:, G * j : G * (j + 1)], banks[2 + j], SIGMOID)
         for h in range(2):
             nc.vector.tensor_copy(window[:].indirect(offsets[:, 16 * h : 16 * (h + 1)]), ys[h][:])
         nc.sync.dma_start(out[0], window[:])

@@ -51,8 +51,7 @@ def tile_attend_residscat_topk_kernel(tc, qT, k_words, k_scales, c_words, c_scal
         planes = keep.tile([P, 2, 2 * N], U8, name="planes", align_bytes=64)
         nc.vector.memset(planes[:, 1, :].bitcast(I32), 0)
         window = keep.tile([P, T], F32, name="window")
-        for i in range(8):
-            nc.gpsimd.memset(window[:, 256 * i : 256 * (i + 1)], 0.0)
+        nc.vector.memset(window[:], 0.0)
 
         s_g = keep.tile([P, 2 * N], U8, name="s_g", align_bytes=64)
         for i in range(2):

@@ -87,14 +87,16 @@ def tile_attend_residscat_topk_kernel(tc, qT, k_words, k_scales, c_words, c_scal
         def part(dst, src):
             nc.vector.tensor_copy(dst.bitcast(U16), src.bitcast(U16).rearrange("p (n h) -> p h n", h=2))
 
-        k_first = keep.tile([P, HALF], U32, name="k_first")
-        late = keep.tile([P, N], U32, name="late")
+        k_g = keep.tile([P, N], U32, name="k_g")
+        late = keep.tile([P, HALF + G], U32, name="late")
         k_split = [keep.tile([P, 2, 2 * HALF], U8, name="k_split%d" % h, align_bytes=64) for h in range(2)]
         c_split = [keep.tile([P, 2, 2 * HALF], U8, name="c_split%d" % h, align_bytes=64) for h in range(2)]
         ys = [keep.tile([P, HALF], F32, name="y%d" % h) for h in range(2)]
 
-        gather(k_first[:], kw, 0)
-        part(k_split[0][:], k_first[:])
+        for h in range(2):
+            gather(k_g[:, HALF * h : HALF * (h + 1)], kw, h)
+        for h in range(2):
+            part(k_split[h][:], k_g[:, HALF * h : HALF * (h + 1)])
         for g in range(2):
             passes(g, k_split[0], G * g, G * g, True)
         gather(late[:, G : G + HALF], cw, 0)
@@ -103,13 +105,10 @@ def tile_attend_residscat_topk_kernel(tc, qT, k_words, k_scales, c_words, c_scal
             passes(g, c_split[0], G * g, N + G * g, False)
             nc.scalar.activation(ys[0][:, G * g : G * (g + 1)], banks[g], SIGMOID)
         gather(late[:, 0:HALF], cw, 1)
-        gather(late[:, HALF:N], kw, 1)
         part(c_split[1][:], late[:, 0:HALF])
-        part(k_split[1][:], late[:, HALF:N])
         for j in range(2):
-            passes(2 + j, c_split[1], G * j, N + HALF + G * j, True)
-        for j in range(2):
-            passes(2 + j, k_split[1], G * j, HALF + G * j, False)
+            passes(2 + j, k_split[1], G * j, HALF + G * j, True)
+            passes(2 + j, c_split[1], G * j, N + HALF + G * j, False)
             nc.scalar.activation(ys[1][:, G * j : G * (j + 1)], banks[2 + j], SIGMOID)
         for h in range(2):
             nc.vector.tensor_copy(window[:].indirect(offsets[:, 16 * h : 16 * (h + 1)]), ys[h][:])

@@ -10,6 +10,7 @@ U16 = mybir.dt.uint16
 U8 = mybir.dt.uint8
 FP8X4 = mybir.dt.float8_e4m3fn_x4
 FP4X4 = mybir.dt.float4_e2m1fn_x4
+ADD = mybir.AluOpType.add
 SIGMOID = mybir.ActivationFunctionType.Sigmoid
 
 P = 128
@@ -50,10 +51,12 @@ def tile_attend_residscat_topk_kernel(tc, qT, k_words, k_scales, c_words, c_scal
         nc.scalar.activation(warm[:, 1:2], warm[:, 0:1], SIGMOID)
         planes = keep.tile([P, 2, 2 * N], U8, name="planes", align_bytes=64)
         nc.vector.memset(planes[:, 1, :].bitcast(I32), 0)
+        zeros = keep.tile([P, G], F32, name="zeros")
+        nc.vector.memset(zeros[:], 0.0)
         window = keep.tile([P, T], F32, name="window")
         nc.vector.memset(window[:], 0.0)
 
-        s_g = keep.tile([P, 2 * N], U8, name="s_g", align_bytes=64)
+        s_g = keep.tile([P, 2 * N], U8, name="s_g", tag="s_then_c", align_bytes=64)
         for i in range(2):
             nc.vector.tensor_copy(s_g[:, i * N : (i + 1) * N], s_wins[i][:].indirect(offsets[:]))
         nc.vector.tensor_copy(planes[:, 0, :].bitcast(I32), s_g[:].bitcast(I32))
@@ -70,8 +73,8 @@ def tile_attend_residscat_topk_kernel(tc, qT, k_words, k_scales, c_words, c_scal
 
         nc.vector.quantize_mx(q_codes[:].bitcast(FP8X4), q_plane[:], q_bf[:].rearrange("p o n j -> p (o n j)"))
 
-        pair = [psum.tile([P, 2, G], F32, name="bank%d" % j) for j in range(2)]
-        banks = [pair[g % 2][:, g // 2, :] for g in range(4)]
+        bank_tiles = [psum.tile([P, G], F32, name="bank%d" % g) for g in range(4)]
+        banks = [b[:] for b in bank_tiles]
 
         def passes(g, words, col, plane_col, first):
             for o in (1, 0):
@@ -88,28 +91,31 @@ def tile_attend_residscat_topk_kernel(tc, qT, k_words, k_scales, c_words, c_scal
             nc.vector.tensor_copy(dst.bitcast(U16), src.bitcast(U16).rearrange("p (n h) -> p h n", h=2))
 
         k_g = keep.tile([P, N], U32, name="k_g")
-        late = keep.tile([P, HALF + G], U32, name="late")
+        c_first = keep.tile([P, HALF], U32, name="c_first")
         k_split = [keep.tile([P, 2, 2 * HALF], U8, name="k_split%d" % h, align_bytes=64) for h in range(2)]
         c_split = [keep.tile([P, 2, 2 * HALF], U8, name="c_split%d" % h, align_bytes=64) for h in range(2)]
-        ys = [keep.tile([P, HALF], F32, name="y%d" % h) for h in range(2)]
+        y_first = keep.tile([P, G], F32, name="y_first")
+        y_rest = keep.tile([P, N - G], F32, name="y_rest")
+        y_of = [y_first[:]] + [y_rest[:, G * j : G * (j + 1)] for j in range(3)]
 
         for h in range(2):
             gather(k_g[:, HALF * h : HALF * (h + 1)], kw, h)
         for h in range(2):
             part(k_split[h][:], k_g[:, HALF * h : HALF * (h + 1)])
+        for g in range(4):
+            passes(g, k_split[g // 2], G * (g % 2), G * g, True)
+        gather(c_first[:], cw, 0)
+        c_second = keep.tile([P, HALF], U32, name="c_second", tag="s_then_c", align_bytes=64)
         for g in range(2):
-            passes(g, k_split[0], G * g, G * g, True)
-        gather(late[:, G : G + HALF], cw, 0)
-        for g in range(2):
-            part(c_split[0][:, :, 2 * G * g : 2 * G * (g + 1)], late[:, G * (g + 1) : G * (g + 2)])
+            part(c_split[0][:, :, 2 * G * g : 2 * G * (g + 1)], c_first[:, G * g : G * (g + 1)])
+            if g == 0:
+                gather(c_second[:], cw, 1)
             passes(g, c_split[0], G * g, N + G * g, False)
-            nc.scalar.activation(ys[0][:, G * g : G * (g + 1)], banks[g], SIGMOID)
-        gather(late[:, 0:HALF], cw, 1)
-        part(c_split[1][:], late[:, 0:HALF])
+            nc.scalar.activation(y_of[g], banks[g], SIGMOID)
         for j in range(2):
-            passes(2 + j, k_split[1], G * j, HALF + G * j, True)
+            part(c_split[1][:, :, 2 * G * j : 2 * G * (j + 1)], c_second[:, G * j : G * (j + 1)])
             passes(2 + j, c_split[1], G * j, N + HALF + G * j, False)
-            nc.scalar.activation(ys[1][:, G * j : G * (j + 1)], banks[2 + j], SIGMOID)
-        for h in range(2):
-            nc.vector.tensor_copy(window[:].indirect(offsets[:, 16 * h : 16 * (h + 1)]), ys[h][:])
+            nc.scalar.activation(y_of[2 + j], banks[2 + j], SIGMOID)
+        nc.vector.tensor_tensor(window[:].indirect(offsets[:, 0:8]), y_first[:], zeros[:], ADD)
+        nc.vector.tensor_copy(window[:].indirect(offsets[:, 8:32]), y_rest[:])
         nc.sync.dma_start(out[0], window[:])

@@ -34,8 +34,9 @@ def tile_attend_residscat_topk_kernel(tc, qT, k_words, k_scales, c_words, c_scal
 
         kw = keep.tile([P, T], I32, name="kw")
         cw = keep.tile([P, T], I32, name="cw")
-        q_raw = keep.tile([P, 2, 4, NQ], F32, name="q_raw")
-        nc.scalar.dma_start(q_raw[:], qT[0].rearrange("(o p j) n -> p o j n", o=2, j=4))
+        q_rows = qT[0].rearrange("(o p j) n -> o p j n", o=2, j=4)
+        q_raw = [keep.tile([P, 4, NQ], F32, name="q_raw%d" % o) for o in range(2)]
+        nc.scalar.dma_start(q_raw[1][:], q_rows[1])
         s_wins = []
         for name, scales in (("ks_win", k_scales), ("cs_win", c_scales)):
             win = keep.tile([P, T], U8, name=name)
@@ -44,15 +45,15 @@ def tile_attend_residscat_topk_kernel(tc, qT, k_words, k_scales, c_words, c_scal
             nc.vector.memset(win[64:128, :].bitcast(I32), 0)
             s_wins.append(win)
         nc.sync.dma_start(kw[:], k_words[0].rearrange("p t b -> p (t b)").bitcast(I32))
+        nc.sync.dma_start(q_raw[0][:], q_rows[0])
         nc.sync.dma_start(cw[:], c_words[0].rearrange("p t b -> p (t b)").bitcast(I32))
 
-        warm = keep.tile([P, 2], F32, name="warm")
-        nc.gpsimd.memset(warm[:, 0:1], 0.0)
-        nc.scalar.activation(warm[:, 1:2], warm[:, 0:1], SIGMOID)
+        zeros = keep.tile([P, G], F32, name="zeros")
+        nc.gpsimd.memset(zeros[:], 0.0)
+        warm = keep.tile([P, 1], F32, name="warm")
+        nc.scalar.activation(warm[:], zeros[:, 0:1], SIGMOID)
         planes = keep.tile([P, 2, 2 * N], U8, name="planes", align_bytes=64)
         nc.vector.memset(planes[:, 1, :].bitcast(I32), 0)
-        zeros = keep.tile([P, G], F32, name="zeros")
-        nc.vector.memset(zeros[:], 0.0)
         window = keep.tile([P, T], F32, name="window")
         nc.vector.memset(window[:], 0.0)
 
@@ -65,21 +66,20 @@ def tile_attend_residscat_topk_kernel(tc, qT, k_words, k_scales, c_words, c_scal
                 nc.sync.dma_start(planes[32 * Q : 32 * Q + 4, o, :].bitcast(I32),
                                   s_g[16 * o + 4 * Q : 16 * o + 4 * Q + 4, :].bitcast(I32))
 
-        q_bf = keep.tile([P, 2, NQ, 4], BF16, name="q_bf", align_bytes=64)
-        for o in range(2):
-            nc.scalar.copy(q_bf[:, o], q_raw[:, o].rearrange("p j n -> p n j"))
-        q_codes = keep.tile([P, 2 * NQ], U32, name="q_codes", align_bytes=64)
-        q_plane = keep.tile([P, 2 * NQ], U8, name="q_plane", align_bytes=64)
-
-        nc.vector.quantize_mx(q_codes[:].bitcast(FP8X4), q_plane[:], q_bf[:].rearrange("p o n j -> p (o n j)"))
+        q_codes = [keep.tile([P, NQ], U32, name="q_codes%d" % o, align_bytes=64) for o in range(2)]
+        q_plane = [keep.tile([P, NQ], U8, name="q_plane%d" % o, align_bytes=64) for o in range(2)]
+        for o in (1, 0):
+            q_bf = keep.tile([P, NQ, 4], BF16, name="q_bf%d" % o, align_bytes=64)
+            nc.scalar.copy(q_bf[:], q_raw[o][:].rearrange("p j n -> p n j"))
+            nc.vector.quantize_mx(q_codes[o][:].bitcast(FP8X4), q_plane[o][:], q_bf[:].rearrange("p n j -> p (n j)"))
 
         bank_tiles = [psum.tile([P, G], F32, name="bank%d" % g) for g in range(4)]
         banks = [b[:] for b in bank_tiles]
 
         def passes(g, words, col, plane_col, first):
             for o in (1, 0):
-                nc.tensor.matmul_mx(banks[g], lhsT=q_codes[:, o * NQ : (o + 1) * NQ].bitcast(FP8X4),
-                                    lhsT_scale=q_plane[:, o * NQ : (o + 1) * NQ],
+                nc.tensor.matmul_mx(banks[g], lhsT=q_codes[o][:].bitcast(FP8X4),
+                                    lhsT_scale=q_plane[o][:],
                                     rhs=words[:, o, 2 * col : 2 * (col + G)].bitcast(FP4X4),
                                     rhs_scale=planes[:, o, plane_col : plane_col + G],
                                     start=(first and o == 1), stop=(not first and o == 0))

@@ -53,14 +53,13 @@ def tile_attend_residscat_topk_kernel(tc, qT, k_words, k_scales, c_words, c_scal
         warm = keep.tile([P, 1], F32, name="warm")
         nc.scalar.activation(warm[:], zeros[:, 0:1], SIGMOID)
         planes = keep.tile([P, 2, 2 * N], U8, name="planes", align_bytes=64)
-        nc.vector.memset(planes[:, 1, :].bitcast(I32), 0)
+        nc.vector.memset(planes[:].rearrange("p o n -> p (o n)").bitcast(I32), 0)
         window = keep.tile([P, T], F32, name="window")
-        nc.vector.memset(window[:], 0.0)
 
         s_g = keep.tile([P, 2 * N], U8, name="s_g", tag="s_then_c", align_bytes=64)
         for i in range(2):
             nc.vector.tensor_copy(s_g[:, i * N : (i + 1) * N], s_wins[i][:].indirect(offsets[:]))
-        nc.vector.tensor_copy(planes[:, 0, :].bitcast(I32), s_g[:].bitcast(I32))
+        nc.vector.tensor_copy(planes[0:32, 0, :].bitcast(I32), s_g[0:32, :].bitcast(I32))
         for o in (1, 0):
             for Q in range(1 - o, 4):
                 nc.sync.dma_start(planes[32 * Q : 32 * Q + 4, o, :].bitcast(I32),
@@ -102,7 +101,7 @@ def tile_attend_residscat_topk_kernel(tc, qT, k_words, k_scales, c_words, c_scal
             gather(k_g[:, HALF * h : HALF * (h + 1)], kw, h)
         for h in range(2):
             part(k_split[h][:], k_g[:, HALF * h : HALF * (h + 1)])
-        for g in range(4):
+        for g in range(2):
             passes(g, k_split[g // 2], G * (g % 2), G * g, True)
         gather(c_first[:], cw, 0)
         c_second = keep.tile([P, HALF], U32, name="c_second", tag="s_then_c", align_bytes=64)
@@ -112,10 +111,14 @@ def tile_attend_residscat_topk_kernel(tc, qT, k_words, k_scales, c_words, c_scal
                 gather(c_second[:], cw, 1)
             passes(g, c_split[0], G * g, N + G * g, False)
             nc.scalar.activation(y_of[g], banks[g], SIGMOID)
+        for g in (2, 3):
+            passes(g, k_split[g // 2], G * (g % 2), G * g, True)
         for j in range(2):
             part(c_split[1][:, :, 2 * G * j : 2 * G * (j + 1)], c_second[:, G * j : G * (j + 1)])
             passes(2 + j, c_split[1], G * j, N + HALF + G * j, False)
             nc.scalar.activation(y_of[2 + j], banks[2 + j], SIGMOID)
+        for i in range(4):
+            nc.vector.memset(window[:, N * i : N * (i + 1)], 0.0)
         nc.vector.tensor_tensor(window[:].indirect(offsets[:, 0:8]), y_first[:], zeros[:], ADD)
         nc.vector.tensor_copy(window[:].indirect(offsets[:, 8:32]), y_rest[:])
         nc.sync.dma_start(out[0], window[:])

@@ -39,10 +39,9 @@ def tile_attend_residscat_topk_kernel(tc, qT, k_words, k_scales, c_words, c_scal
         nc.scalar.dma_start(q_raw[1][:], q_rows[1])
         s_wins = []
         for name, scales in (("ks_win", k_scales), ("cs_win", c_scales)):
-            win = keep.tile([P, T], U8, name=name)
-            nc.sync.dma_start(win[0:32, :].bitcast(I32), scales.rearrange("o f t -> (o f) t").bitcast(I32))
-            nc.vector.memset(win[32:64, :].bitcast(I32), 0)
-            nc.vector.memset(win[64:128, :].bitcast(I32), 0)
+            win = keep.tile([P, T], U8, name=name, tag=name, align_bytes=64)
+            nc.sync.dma_start(win[96:128, :].bitcast(I32), scales.bitcast(I32).rearrange("o f t -> f o t"))
+            nc.vector.memset(win[0:96, :].bitcast(I32), 0)
             s_wins.append(win)
         nc.sync.dma_start(kw[:], k_words[0].rearrange("p t b -> p (t b)").bitcast(I32))
         nc.sync.dma_start(q_raw[0][:], q_rows[0])
@@ -52,18 +51,15 @@ def tile_attend_residscat_topk_kernel(tc, qT, k_words, k_scales, c_words, c_scal
         nc.gpsimd.memset(zeros[:], 0.0)
         warm = keep.tile([P, 1], F32, name="warm")
         nc.scalar.activation(warm[:], zeros[:, 0:1], SIGMOID)
-        planes = keep.tile([P, 2, 2 * N], U8, name="planes", align_bytes=64)
-        nc.vector.memset(planes[:].rearrange("p o n -> p (o n)").bitcast(I32), 0)
         window = keep.tile([P, T], F32, name="window")
 
         s_g = keep.tile([P, 2 * N], U8, name="s_g", tag="s_then_c", align_bytes=64)
         for i in range(2):
             nc.vector.tensor_copy(s_g[:, i * N : (i + 1) * N], s_wins[i][:].indirect(offsets[:]))
-        nc.vector.tensor_copy(planes[0:32, 0, :].bitcast(I32), s_g[0:32, :].bitcast(I32))
-        for o in (1, 0):
-            for Q in range(1 - o, 4):
-                nc.sync.dma_start(planes[32 * Q : 32 * Q + 4, o, :].bitcast(I32),
-                                  s_g[16 * o + 4 * Q : 16 * o + 4 * Q + 4, :].bitcast(I32))
+        planes = keep.tile([P, 2, 2 * N], U8, name="planes", tag="ks_win", align_bytes=64)
+        for Q in range(4):
+            nc.sync.dma_start(planes[32 * Q : 32 * Q + 4, :, :].bitcast(I32),
+                              s_g[96 + 8 * Q : 96 + 8 * Q + 8, :].bitcast(I32))
 
         q_codes = [keep.tile([P, NQ], U32, name="q_codes%d" % o, align_bytes=64) for o in range(2)]
         q_plane = [keep.tile([P, NQ], U8, name="q_plane%d" % o, align_bytes=64) for o in range(2)]

@@ -49,8 +49,6 @@ def tile_attend_residscat_topk_kernel(tc, qT, k_words, k_scales, c_words, c_scal
 
         zeros = keep.tile([P, G], F32, name="zeros")
         nc.gpsimd.memset(zeros[:], 0.0)
-        warm = keep.tile([P, 1], F32, name="warm")
-        nc.scalar.activation(warm[:], zeros[:, 0:1], SIGMOID)
         window = keep.tile([P, T], F32, name="window")
 
         s_g = keep.tile([P, 2 * N], U8, name="s_g", tag="s_then_c", align_bytes=64)

@@ -21,6 +21,9 @@ D = 1024
 FLOPS = 2 * 2 * D * NQ * N
 HALF = N // 2
 G = 128
+PER_COLUMN = 16
+ROWS_AT = 96
+PASSES = (1, 0)
 
 
 def tile_attend_residscat_topk_kernel(tc, qT, k_words, k_scales, c_words, c_scales, offs, out):
@@ -29,90 +32,102 @@ def tile_attend_residscat_topk_kernel(tc, qT, k_words, k_scales, c_words, c_scal
         keep = ctx.enter_context(tc.tile_pool(name="keep", bufs=1))
         psum = ctx.enter_context(tc.psum_pool(name="psum", bufs=1))
 
-        offsets = keep.tile([P, N // 16], U16, name="offsets")
+        offsets = keep.tile([P, N // PER_COLUMN], U16, name="offsets")
         nc.sync.dma_start(offsets[:], offs)
 
-        kw = keep.tile([P, T], I32, name="kw")
-        cw = keep.tile([P, T], I32, name="cw")
-        q_rows = qT[0].rearrange("(o p j) n -> o p j n", o=2, j=4)
+        k_pool = keep.tile([P, T], I32, name="k_pool")
+        c_pool = keep.tile([P, T], I32, name="c_pool")
+        q_rows = qT[0].rearrange("(o p t) n -> o p t n", o=2, t=4)
         q_raw = [keep.tile([P, 4, NQ], F32, name="q_raw%d" % o) for o in range(2)]
         nc.scalar.dma_start(q_raw[1][:], q_rows[1])
-        s_wins = []
-        for name, scales in (("ks_win", k_scales), ("cs_win", c_scales)):
-            win = keep.tile([P, T], U8, name=name, tag=name, align_bytes=64)
-            nc.sync.dma_start(win[96:128, :].bitcast(I32), scales.bitcast(I32).rearrange("o f t -> f o t"))
-            nc.vector.memset(win[0:96, :].bitcast(I32), 0)
-            s_wins.append(win)
-        nc.sync.dma_start(kw[:], k_words[0].rearrange("p t b -> p (t b)").bitcast(I32))
+        scale_pools = []
+        for name, scales in (("k_scale_pool", k_scales), ("c_scale_pool", c_scales)):
+            scale_pool = keep.tile([P, T], U8, name=name, tag=name, align_bytes=64)
+            nc.sync.dma_start(scale_pool[ROWS_AT:P, :].bitcast(I32), scales.bitcast(I32).rearrange("o f t -> f o t"))
+            nc.vector.memset(scale_pool[0:ROWS_AT, :].bitcast(I32), 0)
+            scale_pools.append(scale_pool)
+        nc.sync.dma_start(k_pool[:], k_words[0].rearrange("p t b -> p (t b)").bitcast(I32))
         nc.sync.dma_start(q_raw[0][:], q_rows[0])
-        nc.sync.dma_start(cw[:], c_words[0].rearrange("p t b -> p (t b)").bitcast(I32))
+        nc.sync.dma_start(c_pool[:], c_words[0].rearrange("p t b -> p (t b)").bitcast(I32))
 
         zeros = keep.tile([P, G], F32, name="zeros")
         nc.gpsimd.memset(zeros[:], 0.0)
         window = keep.tile([P, T], F32, name="window")
 
-        s_g = keep.tile([P, 2 * N], U8, name="s_g", tag="s_then_c", align_bytes=64)
-        for i in range(2):
-            nc.vector.tensor_copy(s_g[:, i * N : (i + 1) * N], s_wins[i][:].indirect(offsets[:]))
-        planes = keep.tile([P, 2, 2 * N], U8, name="planes", tag="ks_win", align_bytes=64)
+        listed_scales = keep.tile([P, 2 * N], U8, name="listed_scales", tag="scales_then_c", align_bytes=64)
+        for table in range(2):
+            nc.vector.tensor_copy(listed_scales[:, table * N : (table + 1) * N],
+                                  scale_pools[table][:].indirect(offsets[:]))
+        planes = keep.tile([P, 2, 2 * N], U8, name="planes", tag="k_scale_pool", align_bytes=64)
         for Q in range(4):
             nc.sync.dma_start(planes[32 * Q : 32 * Q + 4, :, :].bitcast(I32),
-                              s_g[96 + 8 * Q : 96 + 8 * Q + 8, :].bitcast(I32))
+                              listed_scales[ROWS_AT + 8 * Q : ROWS_AT + 8 * Q + 8, :].bitcast(I32))
 
         q_codes = [keep.tile([P, NQ], U32, name="q_codes%d" % o, align_bytes=64) for o in range(2)]
         q_plane = [keep.tile([P, NQ], U8, name="q_plane%d" % o, align_bytes=64) for o in range(2)]
-        for o in (1, 0):
+        for o in PASSES:
             q_bf = keep.tile([P, NQ, 4], BF16, name="q_bf%d" % o, align_bytes=64)
-            nc.scalar.copy(q_bf[:], q_raw[o][:].rearrange("p j n -> p n j"))
-            nc.vector.quantize_mx(q_codes[o][:].bitcast(FP8X4), q_plane[o][:], q_bf[:].rearrange("p n j -> p (n j)"))
+            nc.scalar.copy(q_bf[:], q_raw[o][:].rearrange("p t n -> p n t"))
+            nc.vector.quantize_mx(q_codes[o][:].bitcast(FP8X4), q_plane[o][:], q_bf[:].rearrange("p n t -> p (n t)"))
 
-        bank_tiles = [psum.tile([P, G], F32, name="bank%d" % g) for g in range(4)]
-        banks = [b[:] for b in bank_tiles]
+        banks = [psum.tile([P, G], F32, name="bank%d" % g) for g in range(4)]
 
-        def passes(g, words, col, plane_col, first):
-            for o in (1, 0):
-                nc.tensor.matmul_mx(banks[g], lhsT=q_codes[o][:].bitcast(FP8X4),
+        def multiply(g, table, parted, opens):
+            col = G * (g % 2)
+            for o in PASSES:
+                nc.tensor.matmul_mx(banks[g][:], lhsT=q_codes[o][:].bitcast(FP8X4),
                                     lhsT_scale=q_plane[o][:],
-                                    rhs=words[:, o, 2 * col : 2 * (col + G)].bitcast(FP4X4),
-                                    rhs_scale=planes[:, o, plane_col : plane_col + G],
-                                    start=(first and o == 1), stop=(not first and o == 0))
+                                    rhs=parted[g // 2][:, o, 2 * col : 2 * (col + G)].bitcast(FP4X4),
+                                    rhs_scale=planes[:, o, table * N + G * g : table * N + G * (g + 1)],
+                                    start=(opens and o == PASSES[0]), stop=(not opens and o == PASSES[1]))
 
-        def gather(dst, pool_words, h):
-            nc.vector.tensor_copy(dst, pool_words[:].bitcast(U32).indirect(offsets[:, 16 * h : 16 * (h + 1)]))
+        def slots(first, count):
+            return offsets[:, first // PER_COLUMN : (first + count) // PER_COLUMN]
+
+        def gather(dst, pool_words, half):
+            nc.vector.tensor_copy(dst, pool_words[:].bitcast(U32).indirect(slots(HALF * half, HALF)))
 
         def part(dst, src):
-            nc.vector.tensor_copy(dst.bitcast(U16), src.bitcast(U16).rearrange("p (n h) -> p h n", h=2))
+            nc.vector.tensor_copy(dst.bitcast(U16), src.bitcast(U16).rearrange("p (n o) -> p o n", o=2))
 
-        k_g = keep.tile([P, N], U32, name="k_g")
+        k_listed = keep.tile([P, N], U32, name="k_listed")
         c_first = keep.tile([P, HALF], U32, name="c_first")
-        k_split = [keep.tile([P, 2, 2 * HALF], U8, name="k_split%d" % h, align_bytes=64) for h in range(2)]
-        c_split = [keep.tile([P, 2, 2 * HALF], U8, name="c_split%d" % h, align_bytes=64) for h in range(2)]
+        k_parted = [keep.tile([P, 2, 2 * HALF], U8, name="k_parted%d" % half, align_bytes=64) for half in range(2)]
+        c_parted = [keep.tile([P, 2, 2 * HALF], U8, name="c_parted%d" % half, align_bytes=64) for half in range(2)]
         y_first = keep.tile([P, G], F32, name="y_first")
         y_rest = keep.tile([P, N - G], F32, name="y_rest")
         y_of = [y_first[:]] + [y_rest[:, G * j : G * (j + 1)] for j in range(3)]
 
-        for h in range(2):
-            gather(k_g[:, HALF * h : HALF * (h + 1)], kw, h)
-        for h in range(2):
-            part(k_split[h][:], k_g[:, HALF * h : HALF * (h + 1)])
+        def part_c(g, listed):
+            col = G * (g % 2)
+            part(c_parted[g // 2][:, :, 2 * col : 2 * (col + G)], listed[:, col : col + G])
+
+        for half in range(2):
+            gather(k_listed[:, HALF * half : HALF * (half + 1)], k_pool, half)
+        for half in range(2):
+            part(k_parted[half][:], k_listed[:, HALF * half : HALF * (half + 1)])
         for g in range(2):
-            passes(g, k_split[g // 2], G * (g % 2), G * g, True)
-        gather(c_first[:], cw, 0)
-        c_second = keep.tile([P, HALF], U32, name="c_second", tag="s_then_c", align_bytes=64)
+            multiply(g, 0, k_parted, True)
+
+        gather(c_first[:], c_pool, 0)
+        c_second = keep.tile([P, HALF], U32, name="c_second", tag="scales_then_c", align_bytes=64)
         for g in range(2):
-            part(c_split[0][:, :, 2 * G * g : 2 * G * (g + 1)], c_first[:, G * g : G * (g + 1)])
+            part_c(g, c_first)
             if g == 0:
-                gather(c_second[:], cw, 1)
-            passes(g, c_split[0], G * g, N + G * g, False)
-            nc.scalar.activation(y_of[g], banks[g], SIGMOID)
-        for g in (2, 3):
-            passes(g, k_split[g // 2], G * (g % 2), G * g, True)
-        for j in range(2):
-            part(c_split[1][:, :, 2 * G * j : 2 * G * (j + 1)], c_second[:, G * j : G * (j + 1)])
-            passes(2 + j, c_split[1], G * j, N + HALF + G * j, False)
-            nc.scalar.activation(y_of[2 + j], banks[2 + j], SIGMOID)
-        for i in range(4):
-            nc.vector.memset(window[:, N * i : N * (i + 1)], 0.0)
-        nc.vector.tensor_tensor(window[:].indirect(offsets[:, 0:8]), y_first[:], zeros[:], ADD)
-        nc.vector.tensor_copy(window[:].indirect(offsets[:, 8:32]), y_rest[:])
+                gather(c_second[:], c_pool, 1)
+            multiply(g, 1, c_parted, False)
+            nc.scalar.activation(y_of[g], banks[g][:], SIGMOID)
+        multiply(2, 0, k_parted, True)
+        part_c(2, c_second)
+        multiply(2, 1, c_parted, False)
+        nc.scalar.activation(y_of[2], banks[2][:], SIGMOID)
+        part_c(3, c_second)
+        multiply(3, 1, c_parted, True)
+        multiply(3, 0, k_parted, False)
+        nc.scalar.activation(y_of[3], banks[3][:], SIGMOID)
+
+        for quarter in range(4):
+            nc.vector.memset(window[:, T // 4 * quarter : T // 4 * (quarter + 1)], 0.0)
+        nc.vector.tensor_tensor(window[:].indirect(slots(0, G)), y_first[:], zeros[:], ADD)
+        nc.vector.tensor_copy(window[:].indirect(slots(G, N - G)), y_rest[:])
         nc.sync.dma_start(out[0], window[:])

@@ -22,7 +22,6 @@ FLOPS = 2 * 2 * D * NQ * N
 HALF = N // 2
 G = 128
 PER_COLUMN = 16
-ROWS_AT = 96
 PASSES = (1, 0)
 
 
@@ -33,7 +32,6 @@ def tile_attend_residscat_topk_kernel(tc, qT, k_words, k_scales, c_words, c_scal
         psum = ctx.enter_context(tc.psum_pool(name="psum", bufs=1))
 
         offsets = keep.tile([P, N // PER_COLUMN], U16, name="offsets")
-        nc.sync.dma_start(offsets[:], offs)
 
         k_pool = keep.tile([P, T], I32, name="k_pool")
         c_pool = keep.tile([P, T], I32, name="c_pool")
@@ -43,8 +41,11 @@ def tile_attend_residscat_topk_kernel(tc, qT, k_words, k_scales, c_words, c_scal
         scale_pools = []
         for name, scales in (("k_scale_pool", k_scales), ("c_scale_pool", c_scales)):
             scale_pool = keep.tile([P, T], U8, name=name, tag=name, align_bytes=64)
-            nc.sync.dma_start(scale_pool[ROWS_AT:P, :].bitcast(I32), scales.bitcast(I32).rearrange("o f t -> f o t"))
-            nc.vector.memset(scale_pool[0:ROWS_AT, :].bitcast(I32), 0)
+            nc.sync.dma_start(scale_pool[0:32, :].bitcast(I32), scales.bitcast(I32).rearrange("o f t -> (o f) t"))
+            nc.vector.memset(scale_pool[32:64, :].bitcast(I32), 0)
+            nc.vector.memset(scale_pool[64:P, :].bitcast(I32), 0)
+            if not scale_pools:
+                nc.sync.dma_start(offsets[:], offs)
             scale_pools.append(scale_pool)
         nc.sync.dma_start(k_pool[:], k_words[0].rearrange("p t b -> p (t b)").bitcast(I32))
         nc.sync.dma_start(q_raw[0][:], q_rows[0])
@@ -58,10 +59,14 @@ def tile_attend_residscat_topk_kernel(tc, qT, k_words, k_scales, c_words, c_scal
         for table in range(2):
             nc.vector.tensor_copy(listed_scales[:, table * N : (table + 1) * N],
                                   scale_pools[table][:].indirect(offsets[:]))
-        planes = keep.tile([P, 2, 2 * N], U8, name="planes", tag="k_scale_pool", align_bytes=64)
-        for Q in range(4):
-            nc.sync.dma_start(planes[32 * Q : 32 * Q + 4, :, :].bitcast(I32),
-                              listed_scales[ROWS_AT + 8 * Q : ROWS_AT + 8 * Q + 8, :].bitcast(I32))
+        planes = [keep.tile([P, 2 * N], U8, name="plane%d" % o, tag=tag, align_bytes=64)
+                  for o, tag in enumerate(("c_scale_pool", "k_scale_pool"))]
+        for r in range(4):
+            nc.sync.dma_start(planes[1][r:P:32, :].bitcast(I32), listed_scales[16 + r : 32 : 4, :].bitcast(I32))
+        for Q in (2, 1, 3):
+            nc.sync.dma_start(planes[0][32 * Q : 32 * Q + 4, :].bitcast(I32),
+                              listed_scales[4 * Q : 4 * Q + 4, :].bitcast(I32))
+        nc.vector.tensor_copy(planes[0][0:32, :].bitcast(I32), listed_scales[0:32, :].bitcast(I32))
 
         q_codes = [keep.tile([P, NQ], U32, name="q_codes%d" % o, align_bytes=64) for o in range(2)]
         q_plane = [keep.tile([P, NQ], U8, name="q_plane%d" % o, align_bytes=64) for o in range(2)]
@@ -72,59 +77,53 @@ def tile_attend_residscat_topk_kernel(tc, qT, k_words, k_scales, c_words, c_scal
 
         banks = [psum.tile([P, G], F32, name="bank%d" % g) for g in range(4)]
 
+        def one_pass(g, table, o, words, start, stop):
+            nc.tensor.matmul_mx(banks[g][:], lhsT=q_codes[o][:].bitcast(FP8X4), lhsT_scale=q_plane[o][:],
+                                rhs=words.bitcast(FP4X4),
+                                rhs_scale=planes[o][:, table * N + G * g : table * N + G * (g + 1)],
+                                start=start, stop=stop)
+
         def multiply(g, table, parted, opens):
-            col = G * (g % 2)
             for o in PASSES:
-                nc.tensor.matmul_mx(banks[g][:], lhsT=q_codes[o][:].bitcast(FP8X4),
-                                    lhsT_scale=q_plane[o][:],
-                                    rhs=parted[g // 2][:, o, 2 * col : 2 * (col + G)].bitcast(FP4X4),
-                                    rhs_scale=planes[:, o, table * N + G * g : table * N + G * (g + 1)],
-                                    start=(opens and o == PASSES[0]), stop=(not opens and o == PASSES[1]))
+                one_pass(g, table, o, parted[:, o, :], opens and o == PASSES[0], not opens and o == PASSES[1])
 
         def slots(first, count):
             return offsets[:, first // PER_COLUMN : (first + count) // PER_COLUMN]
 
-        def gather(dst, pool_words, half):
-            nc.vector.tensor_copy(dst, pool_words[:].bitcast(U32).indirect(slots(HALF * half, HALF)))
+        def gather(dst, pool_words, first, count):
+            nc.vector.tensor_copy(dst, pool_words[:].bitcast(U32).indirect(slots(first, count)))
 
         def part(dst, src):
             nc.vector.tensor_copy(dst.bitcast(U16), src.bitcast(U16).rearrange("p (n o) -> p o n", o=2))
 
         k_listed = keep.tile([P, N], U32, name="k_listed")
-        c_first = keep.tile([P, HALF], U32, name="c_first")
-        k_parted = [keep.tile([P, 2, 2 * HALF], U8, name="k_parted%d" % half, align_bytes=64) for half in range(2)]
-        c_parted = [keep.tile([P, 2, 2 * HALF], U8, name="c_parted%d" % half, align_bytes=64) for half in range(2)]
+        k_parted = keep.tile([P, 2, 2 * N], U8, name="k_parted", align_bytes=64)
+        c_parted = [keep.tile([P, 2, 2 * G], U8, name="c_parted%d" % g, align_bytes=64) for g in range(4)]
         y_first = keep.tile([P, G], F32, name="y_first")
         y_rest = keep.tile([P, N - G], F32, name="y_rest")
         y_of = [y_first[:]] + [y_rest[:, G * j : G * (j + 1)] for j in range(3)]
 
-        def part_c(g, listed):
-            col = G * (g % 2)
-            part(c_parted[g // 2][:, :, 2 * col : 2 * (col + G)], listed[:, col : col + G])
+        def k_of(g):
+            return k_parted[:, :, 2 * G * g : 2 * G * (g + 1)]
 
-        for half in range(2):
-            gather(k_listed[:, HALF * half : HALF * (half + 1)], k_pool, half)
-        for half in range(2):
-            part(k_parted[half][:], k_listed[:, HALF * half : HALF * (half + 1)])
-        for g in range(2):
-            multiply(g, 0, k_parted, True)
+        gather(k_listed[:], k_pool, 0, N)
+        part(k_parted[:], k_listed[:])
+        for g in range(4):
+            multiply(g, 0, k_of(g), True)
 
-        gather(c_first[:], c_pool, 0)
+        c_first = keep.tile([P, HALF], U32, name="c_first")
+        gather(c_first[:], c_pool, 0, HALF)
+        halves = c_first[:, 0:G].bitcast(U16).rearrange("p (n o) -> p o n", o=2)
+        for o in PASSES:
+            nc.vector.tensor_copy(c_parted[0][:, o, :].bitcast(U16), halves[:, o, :])
+        multiply(0, 1, c_parted[0][:], False)
+        nc.scalar.activation(y_of[0], banks[0][:], SIGMOID)
         c_second = keep.tile([P, HALF], U32, name="c_second", tag="scales_then_c", align_bytes=64)
-        for g in range(2):
-            part_c(g, c_first)
-            if g == 0:
-                gather(c_second[:], c_pool, 1)
-            multiply(g, 1, c_parted, False)
+        gather(c_second[:], c_pool, HALF, HALF)
+        for g, listed in ((1, c_first[:, G:HALF]), (2, c_second[:, 0:G]), (3, c_second[:, G:HALF])):
+            part(c_parted[g][:], listed)
+            multiply(g, 1, c_parted[g][:], False)
             nc.scalar.activation(y_of[g], banks[g][:], SIGMOID)
-        multiply(2, 0, k_parted, True)
-        part_c(2, c_second)
-        multiply(2, 1, c_parted, False)
-        nc.scalar.activation(y_of[2], banks[2][:], SIGMOID)
-        part_c(3, c_second)
-        multiply(3, 1, c_parted, True)
-        multiply(3, 0, k_parted, False)
-        nc.scalar.activation(y_of[3], banks[3][:], SIGMOID)
 
         for quarter in range(4):
             nc.vector.memset(window[:, T // 4 * quarter : T // 4 * (quarter + 1)], 0.0)

@@ -32,20 +32,17 @@ def tile_attend_residscat_topk_kernel(tc, qT, k_words, k_scales, c_words, c_scal
         psum = ctx.enter_context(tc.psum_pool(name="psum", bufs=1))
 
         offsets = keep.tile([P, N // PER_COLUMN], U16, name="offsets")
-
         k_pool = keep.tile([P, T], I32, name="k_pool")
         c_pool = keep.tile([P, T], I32, name="c_pool")
         q_rows = qT[0].rearrange("(o p t) n -> o p t n", o=2, t=4)
         q_raw = [keep.tile([P, 4, NQ], F32, name="q_raw%d" % o) for o in range(2)]
-        nc.scalar.dma_start(q_raw[1][:], q_rows[1])
+        nc.sync.dma_start(q_raw[1][:], q_rows[1])
+        nc.sync.dma_start(offsets[:], offs)
         scale_pools = []
         for name, scales in (("k_scale_pool", k_scales), ("c_scale_pool", c_scales)):
             scale_pool = keep.tile([P, T], U8, name=name, tag=name, align_bytes=64)
-            nc.sync.dma_start(scale_pool[0:32, :].bitcast(I32), scales.bitcast(I32).rearrange("o f t -> (o f) t"))
-            nc.vector.memset(scale_pool[32:64, :].bitcast(I32), 0)
-            nc.vector.memset(scale_pool[64:P, :].bitcast(I32), 0)
-            if not scale_pools:
-                nc.sync.dma_start(offsets[:], offs)
+            nc.vector.memset(scale_pool[:].bitcast(I32), 0)
+            nc.sync.dma_start(scale_pool[0:P:4, :].bitcast(I32), scales.bitcast(I32).rearrange("o f t -> f o t"))
             scale_pools.append(scale_pool)
         nc.sync.dma_start(k_pool[:], k_words[0].rearrange("p t b -> p (t b)").bitcast(I32))
         nc.sync.dma_start(q_raw[0][:], q_rows[0])
@@ -61,12 +58,11 @@ def tile_attend_residscat_topk_kernel(tc, qT, k_words, k_scales, c_words, c_scal
                                   scale_pools[table][:].indirect(offsets[:]))
         planes = [keep.tile([P, 2 * N], U8, name="plane%d" % o, tag=tag, align_bytes=64)
                   for o, tag in enumerate(("c_scale_pool", "k_scale_pool"))]
-        for r in range(4):
-            nc.sync.dma_start(planes[1][r:P:32, :].bitcast(I32), listed_scales[16 + r : 32 : 4, :].bitcast(I32))
-        for Q in (2, 1, 3):
-            nc.sync.dma_start(planes[0][32 * Q : 32 * Q + 4, :].bitcast(I32),
-                              listed_scales[4 * Q : 4 * Q + 4, :].bitcast(I32))
-        nc.vector.tensor_copy(planes[0][0:32, :].bitcast(I32), listed_scales[0:32, :].bitcast(I32))
+        nc.vector.tensor_copy(planes[0][:].bitcast(I32), listed_scales[:].bitcast(I32))
+        for o in PASSES:
+            for r in range(1 - o, 4):
+                nc.sync.dma_start(planes[o][r:P:32, :].bitcast(I32),
+                                  listed_scales[8 * r + 4 * o : P : 32, :].bitcast(I32))
 
         q_codes = [keep.tile([P, NQ], U32, name="q_codes%d" % o, align_bytes=64) for o in range(2)]
         q_plane = [keep.tile([P, NQ], U8, name="q_plane%d" % o, align_bytes=64) for o in range(2)]
@@ -109,7 +105,9 @@ def tile_attend_residscat_topk_kernel(tc, qT, k_words, k_scales, c_words, c_scal
         gather(k_listed[:], k_pool, 0, N)
         part(k_parted[:], k_listed[:])
         for g in range(4):
-            multiply(g, 0, k_of(g), True)
+            one_pass(g, 0, 1, k_of(g)[:, 1, :], True, False)
+        for g in range(3):
+            one_pass(g, 0, 0, k_of(g)[:, 0, :], False, False)
 
         c_first = keep.tile([P, HALF], U32, name="c_first")
         gather(c_first[:], c_pool, 0, HALF)
@@ -122,7 +120,10 @@ def tile_attend_residscat_topk_kernel(tc, qT, k_words, k_scales, c_words, c_scal
         gather(c_second[:], c_pool, HALF, HALF)
         for g, listed in ((1, c_first[:, G:HALF]), (2, c_second[:, 0:G]), (3, c_second[:, G:HALF])):
             part(c_parted[g][:], listed)
-            multiply(g, 1, c_parted[g][:], False)
+            one_pass(g, 1, 1, c_parted[g][:, 1, :], False, False)
+            one_pass(g, 1, 0, c_parted[g][:, 0, :], False, g < 3)
+            if g == 3:
+                one_pass(g, 0, 0, k_of(g)[:, 0, :], False, True)
             nc.scalar.activation(y_of[g], banks[g][:], SIGMOID)
 
         for quarter in range(4):

@@ -29,6 +29,7 @@ def tile_attend_residscat_topk_kernel(tc, qT, k_words, k_scales, c_words, c_scal
     nc = tc.nc
     with ExitStack() as ctx:
         keep = ctx.enter_context(tc.tile_pool(name="keep", bufs=1))
+        shared = ctx.enter_context(tc.tile_pool(name="shared", bufs=1))
         psum = ctx.enter_context(tc.psum_pool(name="psum", bufs=1))
 
         offsets = keep.tile([P, N // PER_COLUMN], U16, name="offsets")
@@ -49,10 +50,9 @@ def tile_attend_residscat_topk_kernel(tc, qT, k_words, k_scales, c_words, c_scal
         nc.sync.dma_start(c_pool[:], c_words[0].rearrange("p t b -> p (t b)").bitcast(I32))
 
         zeros = keep.tile([P, G], F32, name="zeros")
-        nc.gpsimd.memset(zeros[:], 0.0)
         window = keep.tile([P, T], F32, name="window")
 
-        listed_scales = keep.tile([P, 2 * N], U8, name="listed_scales", tag="scales_then_c", align_bytes=64)
+        listed_scales = shared.tile([P, 2 * N], U8, name="listed_scales", offset=N, align_bytes=64)
         for table in range(2):
             nc.vector.tensor_copy(listed_scales[:, table * N : (table + 1) * N],
                                   scale_pools[table][:].indirect(offsets[:]))
@@ -94,7 +94,8 @@ def tile_attend_residscat_topk_kernel(tc, qT, k_words, k_scales, c_words, c_scal
 
         k_listed = keep.tile([P, N], U32, name="k_listed")
         k_parted = keep.tile([P, 2, 2 * N], U8, name="k_parted", align_bytes=64)
-        c_parted = [keep.tile([P, 2, 2 * G], U8, name="c_parted%d" % g, align_bytes=64) for g in range(4)]
+        c_parted = [shared.tile([P, 2, 2 * G], U8, name="c_parted1", offset=2 * N, align_bytes=64) if g == 1 else
+                    keep.tile([P, 2, 2 * G], U8, name="c_parted%d" % g, align_bytes=64) for g in range(4)]
         y_first = keep.tile([P, G], F32, name="y_first")
         y_rest = keep.tile([P, N - G], F32, name="y_rest")
         y_of = [y_first[:]] + [y_rest[:, G * j : G * (j + 1)] for j in range(3)]
@@ -106,7 +107,7 @@ def tile_attend_residscat_topk_kernel(tc, qT, k_words, k_scales, c_words, c_scal
         part(k_parted[:], k_listed[:])
         for g in range(4):
             one_pass(g, 0, 1, k_of(g)[:, 1, :], True, False)
-        for g in range(3):
+        for g in range(4):
             one_pass(g, 0, 0, k_of(g)[:, 0, :], False, False)
 
         c_first = keep.tile([P, HALF], U32, name="c_first")
@@ -116,18 +117,16 @@ def tile_attend_residscat_topk_kernel(tc, qT, k_words, k_scales, c_words, c_scal
             nc.vector.tensor_copy(c_parted[0][:, o, :].bitcast(U16), halves[:, o, :])
         multiply(0, 1, c_parted[0][:], False)
         nc.scalar.activation(y_of[0], banks[0][:], SIGMOID)
-        c_second = keep.tile([P, HALF], U32, name="c_second", tag="scales_then_c", align_bytes=64)
+        c_second = shared.tile([P, HALF], U32, name="c_second", offset=0, align_bytes=64)
         gather(c_second[:], c_pool, HALF, HALF)
         for g, listed in ((1, c_first[:, G:HALF]), (2, c_second[:, 0:G]), (3, c_second[:, G:HALF])):
             part(c_parted[g][:], listed)
-            one_pass(g, 1, 1, c_parted[g][:, 1, :], False, False)
-            one_pass(g, 1, 0, c_parted[g][:, 0, :], False, g < 3)
-            if g == 3:
-                one_pass(g, 0, 0, k_of(g)[:, 0, :], False, True)
+            multiply(g, 1, c_parted[g][:], False)
             nc.scalar.activation(y_of[g], banks[g][:], SIGMOID)
 
         for quarter in range(4):
             nc.vector.memset(window[:, T // 4 * quarter : T // 4 * (quarter + 1)], 0.0)
+        nc.vector.memset(zeros[:], 0.0)
         nc.vector.tensor_tensor(window[:].indirect(slots(0, G)), y_first[:], zeros[:], ADD)
         nc.vector.tensor_copy(window[:].indirect(slots(G, N - G)), y_rest[:])
         nc.sync.dma_start(out[0], window[:])

@@ -45,8 +45,9 @@ def tile_attend_residscat_topk_kernel(tc, qT, k_words, k_scales, c_words, c_scal
             nc.vector.memset(scale_pool[:].bitcast(I32), 0)
             nc.sync.dma_start(scale_pool[0:P:4, :].bitcast(I32), scales.bitcast(I32).rearrange("o f t -> f o t"))
             scale_pools.append(scale_pool)
+            if name == "k_scale_pool":
+                nc.sync.dma_start(q_raw[0][:], q_rows[0])
         nc.sync.dma_start(k_pool[:], k_words[0].rearrange("p t b -> p (t b)").bitcast(I32))
-        nc.sync.dma_start(q_raw[0][:], q_rows[0])
         nc.sync.dma_start(c_pool[:], c_words[0].rearrange("p t b -> p (t b)").bitcast(I32))
 
         zeros = keep.tile([P, G], F32, name="zeros")
@@ -103,8 +104,10 @@ def tile_attend_residscat_topk_kernel(tc, qT, k_words, k_scales, c_words, c_scal
         def k_of(g):
             return k_parted[:, :, 2 * G * g : 2 * G * (g + 1)]
 
-        gather(k_listed[:], k_pool, 0, N)
-        part(k_parted[:], k_listed[:])
+        for h in range(2):
+            gather(k_listed[:, HALF * h : HALF * (h + 1)], k_pool, HALF * h, HALF)
+        for h in range(2):
+            part(k_parted[:, :, N * h : N * (h + 1)], k_listed[:, HALF * h : HALF * (h + 1)])
         for g in range(4):
             one_pass(g, 0, 1, k_of(g)[:, 1, :], True, False)
         for g in range(4):

@@ -114,7 +114,8 @@ def tile_attend_residscat_topk_kernel(tc, qT, k_words, k_scales, c_words, c_scal
             one_pass(g, 0, 0, k_of(g)[:, 0, :], False, False)
 
         c_first = keep.tile([P, HALF], U32, name="c_first")
-        gather(c_first[:], c_pool, 0, HALF)
+        for g in range(2):
+            gather(c_first[:, G * g : G * (g + 1)], c_pool, G * g, G)
         halves = c_first[:, 0:G].bitcast(U16).rearrange("p (n o) -> p o n", o=2)
         for o in PASSES:
             nc.vector.tensor_copy(c_parted[0][:, o, :].bitcast(U16), halves[:, o, :])

@@ -29,7 +29,7 @@ def tile_attend_residscat_topk_kernel(tc, qT, k_words, k_scales, c_words, c_scal
     nc = tc.nc
     with ExitStack() as ctx:
         keep = ctx.enter_context(tc.tile_pool(name="keep", bufs=1))
-        shared = ctx.enter_context(tc.tile_pool(name="shared", bufs=1))
+        ring = ctx.enter_context(tc.tile_pool(name="ring", bufs=2))
         psum = ctx.enter_context(tc.psum_pool(name="psum", bufs=1))
 
         offsets = keep.tile([P, N // PER_COLUMN], U16, name="offsets")
@@ -53,7 +53,7 @@ def tile_attend_residscat_topk_kernel(tc, qT, k_words, k_scales, c_words, c_scal
         zeros = keep.tile([P, G], F32, name="zeros")
         window = keep.tile([P, T], F32, name="window")
 
-        listed_scales = shared.tile([P, 2 * N], U8, name="listed_scales", offset=N, align_bytes=64)
+        listed_scales = keep.tile([P, 2 * N], U8, name="listed_scales", align_bytes=64)
         for table in range(2):
             nc.vector.tensor_copy(listed_scales[:, table * N : (table + 1) * N],
                                   scale_pools[table][:].indirect(offsets[:]))
@@ -95,8 +95,7 @@ def tile_attend_residscat_topk_kernel(tc, qT, k_words, k_scales, c_words, c_scal
 
         k_listed = keep.tile([P, N], U32, name="k_listed")
         k_parted = keep.tile([P, 2, 2 * N], U8, name="k_parted", align_bytes=64)
-        c_parted = [shared.tile([P, 2, 2 * G], U8, name="c_parted1", offset=2 * N, align_bytes=64) if g == 1 else
-                    keep.tile([P, 2, 2 * G], U8, name="c_parted%d" % g, align_bytes=64) for g in range(4)]
+        c_parted = [keep.tile([P, 2, 2 * G], U8, name="c_parted%d" % g, align_bytes=64) for g in range(4)]
         y_first = keep.tile([P, G], F32, name="y_first")
         y_rest = keep.tile([P, N - G], F32, name="y_rest")
         y_of = [y_first[:]] + [y_rest[:, G * j : G * (j + 1)] for j in range(3)]
@@ -108,25 +107,30 @@ def tile_attend_residscat_topk_kernel(tc, qT, k_words, k_scales, c_words, c_scal
             gather(k_listed[:, HALF * h : HALF * (h + 1)], k_pool, HALF * h, HALF)
         for h in range(2):
             part(k_parted[:, :, N * h : N * (h + 1)], k_listed[:, HALF * h : HALF * (h + 1)])
-        for g in range(4):
-            one_pass(g, 0, 1, k_of(g)[:, 1, :], True, False)
-        for g in range(4):
-            one_pass(g, 0, 0, k_of(g)[:, 0, :], False, False)
-
-        c_first = keep.tile([P, HALF], U32, name="c_first")
-        for g in range(2):
-            gather(c_first[:, G * g : G * (g + 1)], c_pool, G * g, G)
-        halves = c_first[:, 0:G].bitcast(U16).rearrange("p (n o) -> p o n", o=2)
         for o in PASSES:
-            nc.vector.tensor_copy(c_parted[0][:, o, :].bitcast(U16), halves[:, o, :])
-        multiply(0, 1, c_parted[0][:], False)
-        nc.scalar.activation(y_of[0], banks[0][:], SIGMOID)
-        c_second = shared.tile([P, HALF], U32, name="c_second", offset=0, align_bytes=64)
-        gather(c_second[:], c_pool, HALF, HALF)
-        for g, listed in ((1, c_first[:, G:HALF]), (2, c_second[:, 0:G]), (3, c_second[:, G:HALF])):
-            part(c_parted[g][:], listed)
-            multiply(g, 1, c_parted[g][:], False)
-            nc.scalar.activation(y_of[g], banks[g][:], SIGMOID)
+            for g in (0, 2, 3):
+                one_pass(g, 0, o, k_of(g)[:, o, :], o == PASSES[0], False)
+
+        for pair in range(2):
+            listed = []
+            for g in (2 * pair, 2 * pair + 1):
+                words = ring.tile([P, G], U32, name="c_listed")
+                gather(words[:], c_pool, G * g, G)
+                listed.append(words)
+            for g, words in zip((2 * pair, 2 * pair + 1), listed):
+                if g == 0:
+                    halves = words[:].bitcast(U16).rearrange("p (n o) -> p o n", o=2)
+                    for o in PASSES:
+                        nc.vector.tensor_copy(c_parted[g][:, o, :].bitcast(U16), halves[:, o, :])
+                else:
+                    part(c_parted[g][:], words[:])
+                if g == 1:
+                    for o in reversed(PASSES):
+                        one_pass(g, 1, o, c_parted[g][:, o, :], o == PASSES[1], False)
+                    multiply(g, 0, k_of(g), False)
+                else:
+                    multiply(g, 1, c_parted[g][:], False)
+                nc.scalar.activation(y_of[g], banks[g][:], SIGMOID)
 
         for quarter in range(4):
             nc.vector.memset(window[:, T // 4 * quarter : T // 4 * (quarter + 1)], 0.0)

@@ -12,6 +12,7 @@ FP8X4 = mybir.dt.float8_e4m3fn_x4
 FP4X4 = mybir.dt.float4_e2m1fn_x4
 ADD = mybir.AluOpType.add
 SIGMOID = mybir.ActivationFunctionType.Sigmoid
+COPY = mybir.ActivationFunctionType.Copy
 
 P = 128
 T = 2048
@@ -136,5 +137,5 @@ def tile_attend_residscat_topk_kernel(tc, qT, k_words, k_scales, c_words, c_scal
             nc.vector.memset(window[:, T // 4 * quarter : T // 4 * (quarter + 1)], 0.0)
         nc.vector.memset(zeros[:], 0.0)
         nc.vector.tensor_tensor(window[:].indirect(slots(0, G)), y_first[:], zeros[:], ADD)
-        nc.vector.tensor_copy(window[:].indirect(slots(G, N - G)), y_rest[:])
+        nc.scalar.activation(window[:].indirect(slots(G, N - G)), y_rest[:], COPY)
         nc.sync.dma_start(out[0], window[:])

@@ -22,6 +22,7 @@ D = 1024
 FLOPS = 2 * 2 * D * NQ * N
 HALF = N // 2
 G = 128
+DMA_ALIGN = 256
 PER_COLUMN = 16
 PASSES = (1, 0)
 
@@ -34,15 +35,15 @@ def tile_attend_residscat_topk_kernel(tc, qT, k_words, k_scales, c_words, c_scal
         psum = ctx.enter_context(tc.psum_pool(name="psum", bufs=1))
 
         offsets = keep.tile([P, N // PER_COLUMN], U16, name="offsets")
-        k_pool = keep.tile([P, T], I32, name="k_pool")
-        c_pool = keep.tile([P, T], I32, name="c_pool")
+        k_pool = keep.tile([P, T], I32, name="k_pool", align_bytes=DMA_ALIGN)
+        c_pool = keep.tile([P, T], I32, name="c_pool", align_bytes=DMA_ALIGN)
         q_rows = qT[0].rearrange("(o p t) n -> o p t n", o=2, t=4)
-        q_raw = [keep.tile([P, 4, NQ], F32, name="q_raw%d" % o) for o in range(2)]
+        q_raw = [keep.tile([P, 4, NQ], F32, name="q_raw%d" % o, align_bytes=DMA_ALIGN) for o in range(2)]
         nc.sync.dma_start(q_raw[1][:], q_rows[1])
         nc.sync.dma_start(offsets[:], offs)
         scale_pools = []
         for name, scales in (("k_scale_pool", k_scales), ("c_scale_pool", c_scales)):
-            scale_pool = keep.tile([P, T], U8, name=name, tag=name, align_bytes=64)
+            scale_pool = keep.tile([P, T], U8, name=name, tag=name, align_bytes=DMA_ALIGN)
             nc.vector.memset(scale_pool[:].bitcast(I32), 0)
             nc.sync.dma_start(scale_pool[0:P:4, :].bitcast(I32), scales.bitcast(I32).rearrange("o f t -> f o t"))
             scale_pools.append(scale_pool)
@@ -52,13 +53,13 @@ def tile_attend_residscat_topk_kernel(tc, qT, k_words, k_scales, c_words, c_scal
         nc.sync.dma_start(c_pool[:], c_words[0].rearrange("p t b -> p (t b)").bitcast(I32))
 
         zeros = keep.tile([P, G], F32, name="zeros")
-        window = keep.tile([P, T], F32, name="window")
+        window = keep.tile([P, T], F32, name="window", align_bytes=DMA_ALIGN)
 
-        listed_scales = keep.tile([P, 2 * N], U8, name="listed_scales", align_bytes=64)
+        listed_scales = keep.tile([P, 2 * N], U8, name="listed_scales", align_bytes=DMA_ALIGN)
         for table in range(2):
             nc.vector.tensor_copy(listed_scales[:, table * N : (table + 1) * N],
                                   scale_pools[table][:].indirect(offsets[:]))
-        planes = [keep.tile([P, 2 * N], U8, name="plane%d" % o, tag=tag, align_bytes=64)
+        planes = [keep.tile([P, 2 * N], U8, name="plane%d" % o, tag=tag, align_bytes=DMA_ALIGN)
                   for o, tag in enumerate(("c_scale_pool", "k_scale_pool"))]
         nc.vector.tensor_copy(planes[0][:].bitcast(I32), listed_scales[:].bitcast(I32))
         for o in PASSES:

from contextlib import ExitStack

import concourse.mybir as mybir

F32 = mybir.dt.float32
BF16 = mybir.dt.bfloat16
I32 = mybir.dt.int32
U32 = mybir.dt.uint32
U16 = mybir.dt.uint16
U8 = mybir.dt.uint8
FP8X4 = mybir.dt.float8_e4m3fn_x4
FP4X4 = mybir.dt.float4_e2m1fn_x4
ADD = mybir.AluOpType.add
SIGMOID = mybir.ActivationFunctionType.Sigmoid
COPY = mybir.ActivationFunctionType.Copy

P = 128
T = 2048
N = 512
NQ = 128
D = 1024
FLOPS = 2 * 2 * D * NQ * N
HALF = N // 2
G = 128
DMA_ALIGN = 256
PER_COLUMN = 16
PASSES = (1, 0)


def tile_attend_residscat_topk_kernel(tc, qT, k_words, k_scales, c_words, c_scales, offs, out):
    nc = tc.nc
    with ExitStack() as ctx:
        keep = ctx.enter_context(tc.tile_pool(name="keep", bufs=1))
        ring = ctx.enter_context(tc.tile_pool(name="ring", bufs=2))
        psum = ctx.enter_context(tc.psum_pool(name="psum", bufs=1))

        offsets = keep.tile([P, N // PER_COLUMN], U16, name="offsets")
        k_pool = keep.tile([P, T], I32, name="k_pool", align_bytes=DMA_ALIGN)
        c_pool = keep.tile([P, T], I32, name="c_pool", align_bytes=DMA_ALIGN)
        q_rows = qT[0].rearrange("(o p t) n -> o p t n", o=2, t=4)
        q_raw = [keep.tile([P, 4, NQ], F32, name="q_raw%d" % o, align_bytes=DMA_ALIGN) for o in range(2)]
        nc.sync.dma_start(q_raw[1][:], q_rows[1])
        nc.sync.dma_start(offsets[:], offs)
        scale_pools = []
        for name, scales in (("k_scale_pool", k_scales), ("c_scale_pool", c_scales)):
            scale_pool = keep.tile([P, T], U8, name=name, tag=name, align_bytes=DMA_ALIGN)
            nc.vector.memset(scale_pool[:].bitcast(I32), 0)
            nc.sync.dma_start(scale_pool[0:P:4, :].bitcast(I32), scales.bitcast(I32).rearrange("o f t -> f o t"))
            scale_pools.append(scale_pool)
            if name == "k_scale_pool":
                nc.sync.dma_start(q_raw[0][:], q_rows[0])
        nc.sync.dma_start(k_pool[:], k_words[0].rearrange("p t b -> p (t b)").bitcast(I32))
        nc.sync.dma_start(c_pool[:], c_words[0].rearrange("p t b -> p (t b)").bitcast(I32))

        zeros = keep.tile([P, G], F32, name="zeros")
        window = keep.tile([P, T], F32, name="window", align_bytes=DMA_ALIGN)

        listed_scales = keep.tile([P, 2 * N], U8, name="listed_scales", align_bytes=DMA_ALIGN)
        for table in range(2):
            nc.vector.tensor_copy(listed_scales[:, table * N : (table + 1) * N],
                                  scale_pools[table][:].indirect(offsets[:]))
        planes = [keep.tile([P, 2 * N], U8, name="plane%d" % o, tag=tag, align_bytes=DMA_ALIGN)
                  for o, tag in enumerate(("c_scale_pool", "k_scale_pool"))]
        nc.vector.tensor_copy(planes[0][:].bitcast(I32), listed_scales[:].bitcast(I32))
        for o in PASSES:
            for r in range(1 - o, 4):
                nc.sync.dma_start(planes[o][r:P:32, :].bitcast(I32),
                                  listed_scales[8 * r + 4 * o : P : 32, :].bitcast(I32))

        q_codes = [keep.tile([P, NQ], U32, name="q_codes%d" % o, align_bytes=64) for o in range(2)]
        q_plane = [keep.tile([P, NQ], U8, name="q_plane%d" % o, align_bytes=64) for o in range(2)]
        for o in PASSES:
            q_bf = keep.tile([P, NQ, 4], BF16, name="q_bf%d" % o, align_bytes=64)
            nc.scalar.copy(q_bf[:], q_raw[o][:].rearrange("p t n -> p n t"))
            nc.vector.quantize_mx(q_codes[o][:].bitcast(FP8X4), q_plane[o][:], q_bf[:].rearrange("p n t -> p (n t)"))

        banks = [psum.tile([P, G], F32, name="bank%d" % g) for g in range(4)]

        def one_pass(g, table, o, words, start, stop):
            nc.tensor.matmul_mx(banks[g][:], lhsT=q_codes[o][:].bitcast(FP8X4), lhsT_scale=q_plane[o][:],
                                rhs=words.bitcast(FP4X4),
                                rhs_scale=planes[o][:, table * N + G * g : table * N + G * (g + 1)],
                                start=start, stop=stop)

        def multiply(g, table, parted, opens):
            for o in PASSES:
                one_pass(g, table, o, parted[:, o, :], opens and o == PASSES[0], not opens and o == PASSES[1])

        def slots(first, count):
            return offsets[:, first // PER_COLUMN : (first + count) // PER_COLUMN]

        def gather(dst, pool_words, first, count):
            nc.vector.tensor_copy(dst, pool_words[:].bitcast(U32).indirect(slots(first, count)))

        def part(dst, src):
            nc.vector.tensor_copy(dst.bitcast(U16), src.bitcast(U16).rearrange("p (n o) -> p o n", o=2))

        k_listed = keep.tile([P, N], U32, name="k_listed")
        k_parted = keep.tile([P, 2, 2 * N], U8, name="k_parted", align_bytes=64)
        c_parted = [keep.tile([P, 2, 2 * G], U8, name="c_parted%d" % g, align_bytes=64) for g in range(4)]
        y_first = keep.tile([P, G], F32, name="y_first")
        y_rest = keep.tile([P, N - G], F32, name="y_rest")
        y_of = [y_first[:]] + [y_rest[:, G * j : G * (j + 1)] for j in range(3)]

        def k_of(g):
            return k_parted[:, :, 2 * G * g : 2 * G * (g + 1)]

        for h in range(2):
            gather(k_listed[:, HALF * h : HALF * (h + 1)], k_pool, HALF * h, HALF)
        for h in range(2):
            part(k_parted[:, :, N * h : N * (h + 1)], k_listed[:, HALF * h : HALF * (h + 1)])
        for o in PASSES:
            for g in (0, 2, 3):
                one_pass(g, 0, o, k_of(g)[:, o, :], o == PASSES[0], False)

        for pair in range(2):
            listed = []
            for g in (2 * pair, 2 * pair + 1):
                words = ring.tile([P, G], U32, name="c_listed")
                gather(words[:], c_pool, G * g, G)
                listed.append(words)
            for g, words in zip((2 * pair, 2 * pair + 1), listed):
                if g == 0:
                    halves = words[:].bitcast(U16).rearrange("p (n o) -> p o n", o=2)
                    for o in PASSES:
                        nc.vector.tensor_copy(c_parted[g][:, o, :].bitcast(U16), halves[:, o, :])
                else:
                    part(c_parted[g][:], words[:])
                if g == 1:
                    for o in reversed(PASSES):
                        one_pass(g, 1, o, c_parted[g][:, o, :], o == PASSES[1], False)
                    multiply(g, 0, k_of(g), False)
                else:
                    multiply(g, 1, c_parted[g][:], False)
                nc.scalar.activation(y_of[g], banks[g][:], SIGMOID)

        for quarter in range(4):
            nc.vector.memset(window[:, T // 4 * quarter : T // 4 * (quarter + 1)], 0.0)
        nc.vector.memset(zeros[:], 0.0)
        nc.vector.tensor_tensor(window[:].indirect(slots(0, G)), y_first[:], zeros[:], ADD)
        nc.scalar.activation(window[:].indirect(slots(G, N - G)), y_rest[:], COPY)
        nc.sync.dma_start(out[0], window[:])
